import numpy as np, ml_dtypes
CORES = [9,13,81,85,89,93,97,101,113,117,121,125]
N = 12
GR, GC = 3, 4
L, KA, KB, F = 12, 3, 4, 32
def setup_inputs(rng):
    return {"a": rng.standard_normal((N, 128, KA * 128), dtype=np.float32).astype(ml_dtypes.bfloat16), "b": rng.standard_normal((N, 128, KB * F), dtype=np.float32).astype(ml_dtypes.bfloat16)}
def reference(a, b):
    A, B = a.astype(np.float64), b.astype(np.float64)
    y = np.zeros((N, 128, F))
    for i in range(GR):
        for j in range(GC):
            for k in range(L):
                At = A[i * GC + k // KA][:, 128 * (k % KA):128 * (k % KA) + 128]
                Bt = B[(k // KB) * GC + j][:, F * (k % KB):F * (k % KB) + F]
                y[i * GC + j] += At.T @ Bt
    return {"y": y.astype(ml_dtypes.bfloat16 if a.dtype != np.float64 else np.float64)}

from concourse.bass import DstId, RemoteDMATransfer
from concourse.mybir import AluOpType

GR, GC = 3, 4
L, KA, KB, F = 12, 3, 4, 32
P = 128
HC = 2
HK = HC * KA
BANK = 512

FEED_ENGINES = 4
NEAR_ENGINES = 4
Y_SPLIT = 2

SCRATCH = {
    "ad": ("dram", [P, KA * P], "bfloat16"),
    "bf": ("dram", [P, KB * F], "bfloat16"),
    "bh": ("dram", [2, P, KB * F // 2], "bfloat16"),
    "rf": ("dram", [P, KB * F], "bfloat16"),
    "rh": ("dram", [P, KB * F // 2], "bfloat16"),
    "al": ("sbuf", [P, HK * P], "bfloat16"),
    "bl": ("sbuf", [P, HC * HK * F], "bfloat16"),
    "ps0": ("psum", [P, BANK], "float32"),
    "ps1": ("psum", [P, BANK], "float32"),
    "ys": ("sbuf", [P, HC * F], "bfloat16"),
    "yl": ("sbuf", [P, 2 * F], "bfloat16"),
    "yo": ("sbuf", [P, F], "bfloat16"),
}
SEMAPHORES = ["ldb", "lda", "rl", "aa", "b0", "b1", "b2", "b3", "mm0", "mm1", "cp", "yy", "ad", "st", "sent"]


def engines(topo, src, dst):
    m = topo.mask(src, dst)
    return [e for e in range(m.bit_length()) if (m >> e) & 1]


def plan(cores, topo):
    every = range(topo.CORES_PER_CHIP * topo.CHIPS)

    def helpers(c):
        far = [d for d in cores if topo.chip(d) != topo.chip(c)]
        return [x for x in every if x not in cores and topo.chip(x) == topo.chip(c)
                and topo.die(x) == topo.die(c) and all(topo.may_write(x, d) for d in far)]

    for i in range(GR):
        for h in range(GC // HC):
            assert topo.chip(cores[i * GC + HC * h]) == topo.chip(cores[i * GC + HC * h + 1])
    main = [helpers(c)[0] for c in cores]
    extra = [helpers(c)[1] for c in cores]
    arrivals = {x: [] for x in main}
    pieces, direct, feeds, jobs = {}, {}, {}, {}
    for s in range(GR * GC):
        r, j = divmod(s, GC)
        q, jj = divmod(j, HC)
        pieces[s] = []
        for h in range(GC // HC):
            ks = [k for k in range(KB * r, KB * r + KB) if k // HK == h]
            if ks:
                pieces[s].append((h, ks))
        direct[s], crossed = [], []
        for p, (h, ks) in enumerate(pieces[s]):
            far = []
            for i in range(GR):
                x = main[i * GC + HC * h + q]
                w = {"piece": p, "dst": x, "col": (jj * HK + ks[0] - HK * h) * F, "width": len(ks) * F,
                     "sem": "b%d" % len(arrivals[x]), "jj": jj, "kl": [k - HK * h for k in ks]}
                arrivals[x].append(w)
                if topo.may_write(cores[s], x):
                    direct[s].append(w)
                else:
                    far.append(w)
            if far:
                crossed.append(far)
        groups = [[w] for w in crossed[0]] if len(crossed) == 1 else sorted(crossed, key=len)
        assert 1 <= len(groups) <= 2
        feeds[s] = []
        for relay, grp in zip((main[s], extra[s]), groups):
            for w in grp:
                w["n"] = len(engines(topo, relay, w["dst"])) // len(grp)
                w["late"] = 1 + len(grp)
            jobs[relay] = grp
            feeds[s].append({"dst": relay, "piece": grp[0]["piece"], "n": FEED_ENGINES // len(groups)})
        off = [w for w in direct[s] if topo.chip(w["dst"]) != topo.chip(cores[s])]
        for w in direct[s]:
            if w in off:
                w["n"] = len(engines(topo, cores[s], w["dst"])) // len(off)
                w["late"] = 1
            else:
                w["n"] = NEAR_ENGINES
                w["late"] = 0
    return main, extra, pieces, direct, feeds, jobs, arrivals


def send(g, T, topo, core, writes):
    used, masks = set(), [0] * len(writes)
    for x in sorted(range(len(writes)), key=lambda x: len(engines(topo, core, writes[x][0]))):
        n = writes[x][4]
        pick = n if isinstance(n, list) else [e for e in engines(topo, core, writes[x][0]) if e not in used][:n]
        assert not used & set(pick)
        used.update(pick)
        masks[x] = sum(1 << e for e in pick)
    trs = []
    for (dst, dap, sap, sem, n), m in zip(writes, masks):
        rid, pid, _ = topo.addr(dst)
        trs.append(RemoteDMATransfer(dst_ids=[DstId(rid=rid, pnc=pid)], dma_engine_mask=m, remote_sem=sem,
                                     src=sap, dst=dap))
    g.remote_dma_fused(trs, local_sem=T.sem.sent)
    return len(used)


def rank_program(g, core, T, topo):
    cores = list(T.cores)
    main, extra, pieces, direct, feeds, jobs, arrivals = plan(cores, topo)
    S = T.sem
    sent = 0

    s = T.rank_of(core)
    if s is not None:
        i, c = divmod(s, GC)
        h = c // HC
        if len(pieces[s]) == 1:
            stage = [T.bf[:, :]]
            g.sync.dma_start(stage[0], T.b[:, :]).then_inc(S.ldb, 16)
            g.scalar.dma_start(T.ad[:, :], T.a[:, :]).then_inc(S.lda, 16)
        else:
            stage = [T.bh[0], T.bh[1]]
            w = KB * F // 2
            g.sync.dma_start(stage[0], T.b[:, 0:w]).then_inc(S.ldb, 16)
            g.scalar.dma_start(stage[1], T.b[:, w:2 * w]).then_inc(S.ldb, 16)
            g.scalar.dma_start(T.ad[:, :], T.a[:, :]).then_inc(S.lda, 16)
        g.wait_ge(S.ldb, 16 * len(stage))
        hold = T.rf[:, :] if len(stage) == 1 else T.rh[:, :]
        sent += send(g, T, topo, core, [(f["dst"], hold, stage[f["piece"]], S.rl, f["n"]) for f in feeds[s]])
        if direct[s]:
            sent += send(g, T, topo, core, [(w["dst"], T.bl[:, w["col"]:w["col"] + w["width"]], stage[w["piece"]],
                                            S[w["sem"]], w["n"]) for w in direct[s]])
        g.wait_ge(S.lda, 16)
        col = (c % HC) * KA * P
        xs = [main[i * GC + HC * h + q] for q in range(HC)]
        xs.sort(key=lambda x: topo.die(x) == topo.die(core))
        sent += send(g, T, topo, core, [(x, T.al[:, col:col + KA * P], T.ad[:, :], S.aa,
                                         engines(topo, core, x)[n::HC]) for n, x in enumerate(xs)])
        ny = 0
        for hh in range(GC // HC):
            x = main[i * GC + HC * hh + c // HC]
            ny += len(engines(topo, x, jobs[x][0]["dst"])) // Y_SPLIT
        g.vector.wait_ge(S.yy, ny)
        g.vector.tensor_tensor(T.yo[:, :], T.yl[:, 0:F], T.yl[:, F:2 * F], AluOpType.add).then_inc(S.ad, 1)
        g.sync.wait_ge(S.ad, 1)
        g.sync.dma_start(T.y[:, :], T.yo[:, :]).then_inc(S.st, 16)
        g.sync.wait_ge(S.st, 16)
        g.wait_ge(S.sent, sent)
        return

    if core not in jobs:
        return

    owner = main.index(core) if core in main else extra.index(core)
    grp = jobs[core]
    feed = [f for f in feeds[owner] if f["dst"] == core][0]
    hold = T.rf[:, :] if len(pieces[owner]) == 1 else T.rh[:, :]
    g.wait_ge(S.rl, feed["n"])
    sent += send(g, T, topo, core, [(w["dst"], T.bl[:, w["col"]:w["col"] + w["width"]], hold, S[w["sem"]], w["n"])
                                    for w in grp])
    if core not in main:
        g.wait_ge(S.sent, sent)
        return

    i, c = divmod(owner, GC)
    h, q = divmod(c, HC)
    ps = [T.ps0, T.ps1]
    mm = [S.mm0, S.mm1]
    na = sum(len(engines(topo, cores[i * GC + HC * h + n], core)) // HC for n in range(HC))
    g.tensor.wait_ge(S.aa, na)
    left = [HK] * HC
    for w in sorted(arrivals[core], key=lambda w: w["late"]):
        g.tensor.wait_ge(S[w["sem"]], w["n"])
        jj = w["jj"]
        for kl in w["kl"]:
            col = (jj * HK + kl) * F
            g.tensor.matmul(ps[jj][:, 0:F], T.al[:, kl * P:(kl + 1) * P], T.bl[:, col:col + F],
                            left[jj] == HK, left[jj] == 1).then_inc(mm[jj], 1)
            left[jj] -= 1
    for jj in range(HC):
        g.vector.wait_ge(mm[jj], HK)
        g.vector.tensor_copy(T.ys[:, jj * F:(jj + 1) * F], ps[jj][:, 0:F]).then_inc(S.cp, 1)
    g.wait_ge(S.cp, HC)
    warm = len(engines(topo, core, grp[0]["dst"]))
    sent += send(g, T, topo, core, [(cores[i * GC + HC * q + jj], T.yl[:, h * F:(h + 1) * F],
                                     T.ys[:, jj * F:(jj + 1) * F], S.yy, warm // Y_SPLIT) for jj in range(HC)])
    g.wait_ge(S.sent, sent)
